import numpy as np
import ml_dtypes


def mxq(x, axis, fmt="e4m3"):
    dtype, down = {"e4m3": (ml_dtypes.float8_e4m3fn, 7), "e5m2": (ml_dtypes.float8_e5m2, 14)}[fmt]
    v = np.moveaxis(np.asarray(x, np.float32).astype(ml_dtypes.bfloat16).astype(np.float64), axis, -1)
    blocks = v.reshape(v.shape[:-1] + (-1, 32))
    amax = np.abs(blocks).max(-1, keepdims=True)
    byte = np.maximum(np.where(amax > 0, np.frexp(amax)[1] - 1 + 127, 0) - down, 1)
    scale = np.exp2(byte - 127.0)
    codes = (blocks / scale).astype(np.float32).astype(dtype).astype(np.float64)
    return np.moveaxis((codes * scale).reshape(v.shape), -1, axis)


WIDE = False


def mx_kscale(k):
    if not WIDE:
        return np.ones(k)
    levels = np.array([10, -10, 5, -5, 0])
    if k % 512:
        return np.exp2(np.random.permutation(np.resize(levels, k // 32))).repeat(32)
    a = np.empty((k // 512, 16))
    for p in range(k // 512):
        a[p, :8] = np.random.permutation(np.resize(levels, 8))
        for g in range(8):
            far = levels[np.abs(levels - a[p, g]) >= 10]
            a[p, g + 8] = far[np.random.randint(len(far))]
    return np.exp2(a.ravel()).repeat(32)


def f64(x):
    return np.asarray(x).astype(np.float64)


def striped(idx):
    return np.tile(idx.reshape(-1, 16).T, (8, 1)).astype(np.uint16)


def unstriped(offs):
    return offs[:16].T.reshape(-1).astype(np.int64)


def pack_weight(w):
    k, n = w.shape
    w = f64(np.asarray(w, np.float32).astype(ml_dtypes.bfloat16)).reshape(k // 32, 32, n)
    amax = np.abs(w).max(1)
    byte = np.clip(np.where(amax > 0, np.frexp(amax)[1] - 1 + 127 - 7, 1), 1, 254)
    scaled = (w * np.exp2(127.0 - byte)[:, None, :]).reshape(k, n).astype(np.float32)
    words = np.ascontiguousarray(scaled.reshape(k // 512, 128, 4, n).transpose(0, 1, 3, 2)).astype(ml_dtypes.float8_e4m3fn).view(np.uint8)
    return words, np.ascontiguousarray(byte.astype(np.uint8).reshape(k // 512, 16, n))


def unpack_weight(words, scales):
    g, p, n, _ = words.shape
    vals = np.ascontiguousarray(words).view(ml_dtypes.float8_e4m3fn).astype(np.float64) * np.repeat(np.exp2(scales.astype(np.float64) - 127.0), 8, axis=1)[..., None]
    return vals.transpose(0, 1, 3, 2).reshape(g * 512, n)


def relu2(v):
    return np.maximum(v, 0.0) ** 2


K, T, E, C, N = 1536, 1024, 8, 128, 512


def by_expert(wq, xq):
    return np.concatenate([wq[e].T @ xq[:, e * C:(e + 1) * C] for e in range(E)], axis=1)


def setup_inputs():
    n = np.random.standard_normal
    s = mx_kscale(K)[:, None]
    packed = [pack_weight(m) for m in n((E, K, N)) / np.sqrt(K) / s[None]]
    return {
        "xT": (n((K, T)) * s).astype(np.float32),
        "w_words": np.stack([m[0] for m in packed]),
        "w_scales": np.stack([m[1] for m in packed]),
        "b": (0.3 * n((N, E))).astype(np.float32),
        "gate": np.tile(np.random.uniform(0.2, 1.0, E * C), (N, 1)).astype(np.float32),
        "offs": striped(np.random.permutation(T)[:E * C]),
        "dst": striped(np.random.permutation(T)[:E * C]),
    }


def reference(xT, w_words, w_scales, b, gate, offs, dst):
    idx = unstriped(offs)
    w = np.stack([unpack_weight(w_words[e], w_scales[e]) for e in range(E)])
    xq = mxq(f64(xT)[:, idx], 0, "e4m3")
    y = by_expert(w, xq)
    y = relu2(y + np.repeat(f64(b), C, axis=1))
    out = np.zeros((N, T))
    out[:, unstriped(dst)] = f64(gate) * y
    return out

@@ -1,0 +1,166 @@
+from contextlib import ExitStack
+
+import concourse.mybir as mybir
+
+K, T, E, C, N = 1536, 1024, 8, 128, 512
+FLOPS = 2 * K * E * C * N
+BYTES = 4 * K * T + E * K * N + E * (K // 32) * N + 4 * N * E + 4 * E * C + 2 * 2 * 128 * (E * C // 16) + 4 * N * T
+
+F32 = mybir.dt.float32
+BF16 = mybir.dt.bfloat16
+I32 = mybir.dt.int32
+U32 = mybir.dt.uint32
+U16 = mybir.dt.uint16
+U8 = mybir.dt.uint8
+FP8X4 = mybir.dt.float8_e4m3fn_x4
+RELU = mybir.ActivationFunctionType.Relu
+SQUARE = mybir.ActivationFunctionType.Square
+COPY = mybir.ActivationFunctionType.Copy
+MULT = mybir.AluOpType.mult
+
+P = 128
+PASSES = K // 512
+HALF = 512
+LIST_HALF = HALF // 16
+EXPERTS_PER_HALF = HALF // C
+
+LOADS = [(0, 0, 512), (0, 512, 512), (1, 0, 512), (1, 512, 512), (2, 0, 512), (2, 512, 256), (2, 768, 256)]
+COPIES = [
+    (0, 0, 256, "v"),
+    (0, 256, 256, "s"),
+    (1, 0, 256, "v"),
+    (1, 256, 256, "s"),
+    (2, 0, 256, "v"),
+    (2, 256, 256, "s"),
+    (3, 0, 256, "v"),
+    (3, 256, 256, "s"),
+    (4, 0, 256, "v"),
+    (4, 256, 256, "s"),
+    (5, 0, 128, "s"),
+    (5, 128, 128, "v"),
+    (6, 0, 128, "s"),
+    (6, 128, 128, "v"),
+]
+
+
+def tile_moe_two_lin_relu2_kernel(tc, xT, w_words, w_scales, b, gate, offs, dst, out):
+    nc = tc.nc
+    with ExitStack() as ctx:
+        lists = ctx.enter_context(tc.tile_pool(name="lists", bufs=1))
+        keep = ctx.enter_context(tc.tile_pool(name="keep", bufs=1))
+        work = ctx.enter_context(tc.tile_pool(name="work", bufs=3))
+        psum = ctx.enter_context(tc.psum_pool(name="psum", bufs=1))
+
+        offs_t = lists.tile([P, T // 16], U16, name="offs_t")
+        dst_t = lists.tile([P, T // 16], U16, name="dst_t")
+
+        w_sc = keep.tile([P, E, N], U8, name="w_sc", align_bytes=64)
+        x_sc = keep.tile([P, T], U8, name="x_sc", align_bytes=64)
+        nc.vector.memset(w_sc[:].rearrange("p e n -> p (e n)").bitcast(I32), 0)
+        nc.gpsimd.memset(x_sc[:], 0)
+
+        sc_view = w_scales.rearrange("e a (q i) n -> a i q e n", i=4)
+
+        def load_scales(queue, rows):
+            for row in rows:
+                queue.dma_start(out=w_sc[row : P : 32, :, :].bitcast(I32), in_=sc_view[row // 4, row % 4].bitcast(I32))
+
+        load_scales(nc.gpsimd, range(6))
+        x_view = xT.rearrange("(a p j) w -> a p j w", p=P, j=4)
+        raws = []
+        for n, (a, c0, width) in enumerate(LOADS):
+            raw = keep.tile([P, 4, width], F32, name="raw%d" % n)
+            nc.sync.dma_start(out=raw[:], in_=x_view[a, :, :, c0 : c0 + width])
+            raws.append(raw)
+            if n == 1:
+                nc.sync.dma_start(offs_t[:], offs)
+                nc.sync.dma_start(dst_t[:], dst)
+            if n == 2:
+                load_scales(nc.sync, range(6, 9))
+            if n == 3:
+                load_scales(nc.sync, range(9, 12))
+
+        bias = keep.tile([P, N // P, E], F32, name="bias")
+        nc.gpsimd.dma_start(out=bias[:], in_=b.rearrange("(g p) e -> p g e", p=P))
+
+        w_view = w_words.rearrange("e a p n r -> p (e a) (n r)")
+        w_tiles = {}
+        gate_t = keep.tile([P, T], F32, name="gate_t")
+        for q in range(2):
+            for pair in range(4):
+                wt = keep.tile([P, 6, 1024], U8, name="w%d_%d" % (q, pair), align_bytes=64)
+                nc.sync.dma_start(
+                    out=wt[:].bitcast(I32), in_=w_view[:, 6 * pair : 6 * pair + 6, 1024 * q : 1024 * q + 1024].bitcast(I32)
+                )
+                w_tiles[q, pair] = wt
+                if q == 0 and pair == 1:
+                    nc.sync.dma_start(out=gate_t[:], in_=gate[0:P, :])
+
+        codes = [keep.tile([P, T], U32, name="codes%d" % a, align_bytes=64) for a in range(PASSES)]
+        g_words = {}
+        g_bytes = {}
+        for h in range(2):
+            for a in range(PASSES):
+                g_words[h, a] = keep.tile([P, HALF], U32, name="gw%d_%d" % (h, a), align_bytes=64)
+            g_bytes[h] = keep.tile([P, HALF], U8, name="gb%d" % h, align_bytes=64)
+
+        def half_list(tile, h):
+            return tile[:, LIST_HALF * h : LIST_HALF * (h + 1)]
+
+        def gather_words(a, h):
+            nc.vector.tensor_copy(g_words[h, a][:], codes[a][:].indirect(half_list(offs_t, h)))
+
+        def gather_bytes(h):
+            nc.vector.tensor_copy(g_bytes[h][:], x_sc[:].indirect(half_list(offs_t, h)))
+
+        for n, (load, l0, width, eng) in enumerate(COPIES):
+            a, c0 = LOADS[load][0], LOADS[load][1] + l0
+            grouped = keep.tile([P, width, 4], BF16, name="grouped%d" % n, align_bytes=64)
+            dst_ap = grouped[:].rearrange("p (c i) t -> p c t i", i=4)
+            src_ap = raws[load][:, :, l0 : l0 + width].rearrange("p t (c i) -> p c t i", i=4)
+            if eng == "v":
+                nc.vector.tensor_copy(out=dst_ap, in_=src_ap)
+            else:
+                nc.scalar.activation(dst_ap, src_ap, COPY)
+            nc.vector.quantize_mx(
+                out=codes[a][:, c0 : c0 + width].bitcast(FP8X4),
+                scales=x_sc[4 * a : P, c0 : c0 + width],
+                in_=grouped[:].rearrange("p w j -> p (w j)"),
+            )
+            if c0 + width == T and a < PASSES - 1:
+                for h in range(2):
+                    gather_words(a, h)
+        for h in range(2):
+            gather_words(PASSES - 1, h)
+            gather_bytes(h)
+
+        windows = [keep.tile([P, T], F32, name="window%d" % g) for g in range(N // P)]
+
+        def block(g, h):
+            bank = psum.tile([P, HALF], F32, name="bank%d_%d" % (g, h))
+            r = work.tile([P, HALF], F32, name="r")
+            for c in range(EXPERTS_PER_HALF):
+                e = EXPERTS_PER_HALF * h + c
+                cols = slice(C * c, C * (c + 1))
+                wt = w_tiles[g // 2, e // 2]
+                for a in range(PASSES):
+                    nc.tensor.matmul_mx(
+                        out=bank[:, cols],
+                        lhsT=wt[:, 3 * (e % 2) + a, 512 * (g % 2) : 512 * (g % 2) + 512].bitcast(FP8X4),
+                        lhsT_scale=w_sc[4 * a : P, e, P * g : P * (g + 1)],
+                        rhs=g_words[h, a][:, cols].bitcast(FP8X4),
+                        rhs_scale=g_bytes[h][4 * a : P, cols],
+                        start=(a == 0),
+                        stop=(a == PASSES - 1),
+                    )
+                nc.scalar.activation(r[:, cols], bank[:, cols], RELU, bias=bias[:, g, e : e + 1])
+            sq = work.tile([P, HALF], F32, name="sq")
+            nc.scalar.activation(sq[:], r[:], SQUARE)
+            nc.vector.tensor_tensor(
+                windows[g][:].indirect(half_list(dst_t, h)), sq[:], gate_t[:, HALF * h : HALF * (h + 1)], MULT
+            )
+            if h == 1:
+                nc.sync.dma_start(out=out[P * g : P * (g + 1), :], in_=windows[g][:])
+
+        for g, h in ((0, 0), (1, 0), (0, 1), (1, 1), (2, 0), (2, 1), (3, 0), (3, 1)):
+            block(g, h)

@@ -24,22 +24,14 @@ HALF = 512
 LIST_HALF = HALF // 16
 EXPERTS_PER_HALF = HALF // C
 
-LOADS = [(0, 0, 512), (0, 512, 512), (1, 0, 512), (1, 512, 512), (2, 0, 512), (2, 512, 256), (2, 768, 256)]
-COPIES = [
-    (0, 0, 256, "v"),
-    (0, 256, 256, "s"),
-    (1, 0, 256, "v"),
-    (1, 256, 256, "s"),
-    (2, 0, 256, "v"),
-    (2, 256, 256, "s"),
-    (3, 0, 256, "v"),
-    (3, 256, 256, "s"),
-    (4, 0, 256, "v"),
-    (4, 256, 256, "s"),
-    (5, 0, 128, "s"),
-    (5, 128, 128, "v"),
-    (6, 0, 128, "s"),
-    (6, 128, 128, "v"),
+LOADS = [
+    (0, 0, 256, 0),
+    (0, 256, 256, 0),
+    (0, 512, 512, 256),
+    (1, 0, 512, 512),
+    (1, 512, 512, 256),
+    (2, 0, 512, 512),
+    (2, 512, 512, 224),
 ]
 
 
@@ -57,7 +49,7 @@ def tile_moe_two_lin_relu2_kernel(tc, xT, w_words, w_scales, b, gate, offs, dst,
         w_sc = keep.tile([P, E, N], U8, name="w_sc", align_bytes=64)
         x_sc = keep.tile([P, T], U8, name="x_sc", align_bytes=64)
         nc.vector.memset(w_sc[:].rearrange("p e n -> p (e n)").bitcast(I32), 0)
-        nc.gpsimd.memset(x_sc[:], 0)
+        nc.vector.memset(x_sc[:].bitcast(I32), 0)
 
         sc_view = w_scales.rearrange("e a (q i) n -> a i q e n", i=4)
 
@@ -65,24 +57,15 @@ def tile_moe_two_lin_relu2_kernel(tc, xT, w_words, w_scales, b, gate, offs, dst,
             for row in rows:
                 queue.dma_start(out=w_sc[row : P : 32, :, :].bitcast(I32), in_=sc_view[row // 4, row % 4].bitcast(I32))
 
-        load_scales(nc.gpsimd, range(6))
+        bias = keep.tile([P, N // P, E], F32, name="bias")
+        load_scales(nc.gpsimd, range(7))
+        nc.sync.dma_start(offs_t[:], offs)
         x_view = xT.rearrange("(a p j) w -> a p j w", p=P, j=4)
         raws = []
-        for n, (a, c0, width) in enumerate(LOADS):
+        for n, (a, c0, width, split) in enumerate(LOADS):
             raw = keep.tile([P, 4, width], F32, name="raw%d" % n)
             nc.sync.dma_start(out=raw[:], in_=x_view[a, :, :, c0 : c0 + width])
             raws.append(raw)
-            if n == 1:
-                nc.sync.dma_start(offs_t[:], offs)
-                nc.sync.dma_start(dst_t[:], dst)
-            if n == 2:
-                load_scales(nc.sync, range(6, 9))
-            if n == 3:
-                load_scales(nc.sync, range(9, 12))
-
-        bias = keep.tile([P, N // P, E], F32, name="bias")
-        nc.gpsimd.dma_start(out=bias[:], in_=b.rearrange("(g p) e -> p g e", p=P))
-
         w_view = w_words.rearrange("e a p n r -> p (e a) (n r)")
         w_tiles = {}
         gate_t = keep.tile([P, T], F32, name="gate_t")
@@ -93,7 +76,11 @@ def tile_moe_two_lin_relu2_kernel(tc, xT, w_words, w_scales, b, gate, offs, dst,
                     out=wt[:].bitcast(I32), in_=w_view[:, 6 * pair : 6 * pair + 6, 1024 * q : 1024 * q + 1024].bitcast(I32)
                 )
                 w_tiles[q, pair] = wt
+                if q == 0 and pair == 0:
+                    load_scales(nc.sync, range(7, 12))
+                    nc.sync.dma_start(out=bias[:], in_=b.rearrange("(g p) e -> p g e", p=P))
                 if q == 0 and pair == 1:
+                    nc.sync.dma_start(dst_t[:], dst)
                     nc.sync.dma_start(out=gate_t[:], in_=gate[0:P, :])
 
         codes = [keep.tile([P, T], U32, name="codes%d" % a, align_bytes=64) for a in range(PASSES)]
@@ -113,15 +100,18 @@ def tile_moe_two_lin_relu2_kernel(tc, xT, w_words, w_scales, b, gate, offs, dst,
         def gather_bytes(h):
             nc.vector.tensor_copy(g_bytes[h][:], x_sc[:].indirect(half_list(offs_t, h)))
 
-        for n, (load, l0, width, eng) in enumerate(COPIES):
-            a, c0 = LOADS[load][0], LOADS[load][1] + l0
+        def interleave(copy, grouped, raw, lo, hi):
+            copy(
+                grouped[:, lo:hi, :].rearrange("p (c i) t -> p c t i", i=4),
+                raw[:, :, lo:hi].rearrange("p t (c i) -> p c t i", i=4),
+            )
+
+        for n, (a, c0, width, split) in enumerate(LOADS):
             grouped = keep.tile([P, width, 4], BF16, name="grouped%d" % n, align_bytes=64)
-            dst_ap = grouped[:].rearrange("p (c i) t -> p c t i", i=4)
-            src_ap = raws[load][:, :, l0 : l0 + width].rearrange("p t (c i) -> p c t i", i=4)
-            if eng == "v":
-                nc.vector.tensor_copy(out=dst_ap, in_=src_ap)
-            else:
-                nc.scalar.activation(dst_ap, src_ap, COPY)
+            if split > 0:
+                interleave(nc.scalar.copy, grouped, raws[n], 0, split)
+            if split < width:
+                interleave(nc.vector.tensor_copy, grouped, raws[n], split, width)
             nc.vector.quantize_mx(
                 out=codes[a][:, c0 : c0 + width].bitcast(FP8X4),
                 scales=x_sc[4 * a : P, c0 : c0 + width],
@@ -136,31 +126,39 @@ def tile_moe_two_lin_relu2_kernel(tc, xT, w_words, w_scales, b, gate, offs, dst,
 
         windows = [keep.tile([P, T], F32, name="window%d" % g) for g in range(N // P)]
 
-        def block(g, h):
-            bank = psum.tile([P, HALF], F32, name="bank%d_%d" % (g, h))
-            r = work.tile([P, HALF], F32, name="r")
-            for c in range(EXPERTS_PER_HALF):
-                e = EXPERTS_PER_HALF * h + c
-                cols = slice(C * c, C * (c + 1))
+        def block(g, e0, count):
+            width = C * count
+            first = C * e0
+            h = first // HALF
+            bank = psum.tile([P, width], F32, name="bank", bufs=8)
+            r = work.tile([P, width], F32, name="r")
+            for c in range(count):
+                e = e0 + c
+                slots = slice(C * e - HALF * h, C * (e + 1) - HALF * h)
                 wt = w_tiles[g // 2, e // 2]
                 for a in range(PASSES):
                     nc.tensor.matmul_mx(
-                        out=bank[:, cols],
+                        out=bank[:, C * c : C * (c + 1)],
                         lhsT=wt[:, 3 * (e % 2) + a, 512 * (g % 2) : 512 * (g % 2) + 512].bitcast(FP8X4),
                         lhsT_scale=w_sc[4 * a : P, e, P * g : P * (g + 1)],
-                        rhs=g_words[h, a][:, cols].bitcast(FP8X4),
-                        rhs_scale=g_bytes[h][4 * a : P, cols],
+                        rhs=g_words[h, a][:, slots].bitcast(FP8X4),
+                        rhs_scale=g_bytes[h][4 * a : P, slots],
                         start=(a == 0),
                         stop=(a == PASSES - 1),
                     )
-                nc.scalar.activation(r[:, cols], bank[:, cols], RELU, bias=bias[:, g, e : e + 1])
-            sq = work.tile([P, HALF], F32, name="sq")
+            for c in range(count):
+                cols = slice(C * c, C * (c + 1))
+                nc.scalar.activation(r[:, cols], bank[:, cols], RELU, bias=bias[:, g, e0 + c : e0 + c + 1])
+            sq = work.tile([P, width], F32, name="sq")
             nc.scalar.activation(sq[:], r[:], SQUARE)
             nc.vector.tensor_tensor(
-                windows[g][:].indirect(half_list(dst_t, h)), sq[:], gate_t[:, HALF * h : HALF * (h + 1)], MULT
+                windows[g][:].indirect(dst_t[:, first // 16 : (first + width) // 16]),
+                sq[:],
+                gate_t[:, first : first + width],
+                MULT,
             )
-            if h == 1:
-                nc.sync.dma_start(out=out[P * g : P * (g + 1), :], in_=windows[g][:])
 
-        for g, h in ((0, 0), (1, 0), (0, 1), (1, 1), (2, 0), (2, 1), (3, 0), (3, 1)):
-            block(g, h)
+        for g, e0, count in ((0, 0, 2), (1, 0, 2), (0, 2, 2), (1, 2, 2), (0, 4, 4), (1, 4, 4), (2, 0, 4), (3, 0, 4), (2, 4, 4), (3, 4, 4)):
+            block(g, e0, count)
+            if e0 + count == E:
+                nc.sync.dma_start(out=out[P * g : P * (g + 1), :], in_=windows[g][:])

from contextlib import ExitStack

import concourse.mybir as mybir

K, T, E, C, N = 1536, 1024, 8, 128, 512
FLOPS = 2 * K * E * C * N
BYTES = 4 * K * T + E * K * N + E * (K // 32) * N + 4 * N * E + 4 * E * C + 2 * 2 * 128 * (E * C // 16) + 4 * N * T

F32 = mybir.dt.float32
BF16 = mybir.dt.bfloat16
I32 = mybir.dt.int32
U32 = mybir.dt.uint32
U16 = mybir.dt.uint16
U8 = mybir.dt.uint8
FP8X4 = mybir.dt.float8_e4m3fn_x4
RELU = mybir.ActivationFunctionType.Relu
SQUARE = mybir.ActivationFunctionType.Square
COPY = mybir.ActivationFunctionType.Copy
MULT = mybir.AluOpType.mult

P = 128
PASSES = K // 512
HALF = 512
LIST_HALF = HALF // 16
EXPERTS_PER_HALF = HALF // C

LOADS = [
    (0, 0, 256, 0),
    (0, 256, 256, 0),
    (0, 512, 512, 256),
    (1, 0, 512, 512),
    (1, 512, 512, 256),
    (2, 0, 512, 512),
    (2, 512, 512, 224),
]


def tile_moe_two_lin_relu2_kernel(tc, xT, w_words, w_scales, b, gate, offs, dst, out):
    nc = tc.nc
    with ExitStack() as ctx:
        lists = ctx.enter_context(tc.tile_pool(name="lists", bufs=1))
        keep = ctx.enter_context(tc.tile_pool(name="keep", bufs=1))
        work = ctx.enter_context(tc.tile_pool(name="work", bufs=3))
        psum = ctx.enter_context(tc.psum_pool(name="psum", bufs=1))

        offs_t = lists.tile([P, T // 16], U16, name="offs_t")
        dst_t = lists.tile([P, T // 16], U16, name="dst_t")

        w_sc = keep.tile([P, E, N], U8, name="w_sc", align_bytes=64)
        x_sc = keep.tile([P, T], U8, name="x_sc", align_bytes=64)
        nc.vector.memset(w_sc[:].rearrange("p e n -> p (e n)").bitcast(I32), 0)
        nc.vector.memset(x_sc[:].bitcast(I32), 0)

        sc_view = w_scales.rearrange("e a (q i) n -> a i q e n", i=4)

        def load_scales(queue, rows):
            for row in rows:
                queue.dma_start(out=w_sc[row : P : 32, :, :].bitcast(I32), in_=sc_view[row // 4, row % 4].bitcast(I32))

        bias = keep.tile([P, N // P, E], F32, name="bias")
        load_scales(nc.gpsimd, range(7))
        nc.sync.dma_start(offs_t[:], offs)
        x_view = xT.rearrange("(a p j) w -> a p j w", p=P, j=4)
        raws = []
        for n, (a, c0, width, split) in enumerate(LOADS):
            raw = keep.tile([P, 4, width], F32, name="raw%d" % n)
            nc.sync.dma_start(out=raw[:], in_=x_view[a, :, :, c0 : c0 + width])
            raws.append(raw)
        w_view = w_words.rearrange("e a p n r -> p (e a) (n r)")
        w_tiles = {}
        gate_t = keep.tile([P, T], F32, name="gate_t")
        for q in range(2):
            for pair in range(4):
                wt = keep.tile([P, 6, 1024], U8, name="w%d_%d" % (q, pair), align_bytes=64)
                nc.sync.dma_start(
                    out=wt[:].bitcast(I32), in_=w_view[:, 6 * pair : 6 * pair + 6, 1024 * q : 1024 * q + 1024].bitcast(I32)
                )
                w_tiles[q, pair] = wt
                if q == 0 and pair == 0:
                    load_scales(nc.sync, range(7, 12))
                    nc.sync.dma_start(out=bias[:], in_=b.rearrange("(g p) e -> p g e", p=P))
                if q == 0 and pair == 1:
                    nc.sync.dma_start(dst_t[:], dst)
                    nc.sync.dma_start(out=gate_t[:], in_=gate[0:P, :])

        codes = [keep.tile([P, T], U32, name="codes%d" % a, align_bytes=64) for a in range(PASSES)]
        g_words = {}
        g_bytes = {}
        for h in range(2):
            for a in range(PASSES):
                g_words[h, a] = keep.tile([P, HALF], U32, name="gw%d_%d" % (h, a), align_bytes=64)
            g_bytes[h] = keep.tile([P, HALF], U8, name="gb%d" % h, align_bytes=64)

        def half_list(tile, h):
            return tile[:, LIST_HALF * h : LIST_HALF * (h + 1)]

        def gather_words(a, h):
            nc.vector.tensor_copy(g_words[h, a][:], codes[a][:].indirect(half_list(offs_t, h)))

        def gather_bytes(h):
            nc.vector.tensor_copy(g_bytes[h][:], x_sc[:].indirect(half_list(offs_t, h)))

        def interleave(copy, grouped, raw, lo, hi):
            copy(
                grouped[:, lo:hi, :].rearrange("p (c i) t -> p c t i", i=4),
                raw[:, :, lo:hi].rearrange("p t (c i) -> p c t i", i=4),
            )

        for n, (a, c0, width, split) in enumerate(LOADS):
            grouped = keep.tile([P, width, 4], BF16, name="grouped%d" % n, align_bytes=64)
            if split > 0:
                interleave(nc.scalar.copy, grouped, raws[n], 0, split)
            if split < width:
                interleave(nc.vector.tensor_copy, grouped, raws[n], split, width)
            nc.vector.quantize_mx(
                out=codes[a][:, c0 : c0 + width].bitcast(FP8X4),
                scales=x_sc[4 * a : P, c0 : c0 + width],
                in_=grouped[:].rearrange("p w j -> p (w j)"),
            )
            if c0 + width == T and a < PASSES - 1:
                for h in range(2):
                    gather_words(a, h)
        for h in range(2):
            gather_words(PASSES - 1, h)
            gather_bytes(h)

        windows = [keep.tile([P, T], F32, name="window%d" % g) for g in range(N // P)]

        def block(g, e0, count):
            width = C * count
            first = C * e0
            h = first // HALF
            bank = psum.tile([P, width], F32, name="bank", bufs=8)
            r = work.tile([P, width], F32, name="r")
            for c in range(count):
                e = e0 + c
                slots = slice(C * e - HALF * h, C * (e + 1) - HALF * h)
                wt = w_tiles[g // 2, e // 2]
                for a in range(PASSES):
                    nc.tensor.matmul_mx(
                        out=bank[:, C * c : C * (c + 1)],
                        lhsT=wt[:, 3 * (e % 2) + a, 512 * (g % 2) : 512 * (g % 2) + 512].bitcast(FP8X4),
                        lhsT_scale=w_sc[4 * a : P, e, P * g : P * (g + 1)],
                        rhs=g_words[h, a][:, slots].bitcast(FP8X4),
                        rhs_scale=g_bytes[h][4 * a : P, slots],
                        start=(a == 0),
                        stop=(a == PASSES - 1),
                    )
            for c in range(count):
                cols = slice(C * c, C * (c + 1))
                nc.scalar.activation(r[:, cols], bank[:, cols], RELU, bias=bias[:, g, e0 + c : e0 + c + 1])
            sq = work.tile([P, width], F32, name="sq")
            nc.scalar.activation(sq[:], r[:], SQUARE)
            nc.vector.tensor_tensor(
                windows[g][:].indirect(dst_t[:, first // 16 : (first + width) // 16]),
                sq[:],
                gate_t[:, first : first + width],
                MULT,
            )

        for g, e0, count in ((0, 0, 2), (1, 0, 2), (0, 2, 2), (1, 2, 2), (0, 4, 4), (1, 4, 4), (2, 0, 4), (3, 0, 4), (2, 4, 4), (3, 4, 4)):
            block(g, e0, count)
            if e0 + count == E:
                nc.sync.dma_start(out=out[P * g : P * (g + 1), :], in_=windows[g][:])
